import numpy as np
import ml_dtypes


def mxq(x, axis, fmt="e4m3"):
    dtype, down = {"e4m3": (ml_dtypes.float8_e4m3fn, 7), "e5m2": (ml_dtypes.float8_e5m2, 14)}[fmt]
    v = np.moveaxis(np.asarray(x, np.float32).astype(ml_dtypes.bfloat16).astype(np.float64), axis, -1)
    blocks = v.reshape(v.shape[:-1] + (-1, 32))
    amax = np.abs(blocks).max(-1, keepdims=True)
    byte = np.maximum(np.where(amax > 0, np.frexp(amax)[1] - 1 + 127, 0) - down, 1)
    scale = np.exp2(byte - 127.0)
    codes = (blocks / scale).astype(np.float32).astype(dtype).astype(np.float64)
    return np.moveaxis((codes * scale).reshape(v.shape), -1, axis)


WIDE = False


def mx_kscale(k):
    if not WIDE:
        return np.ones(k)
    levels = np.array([10, -10, 5, -5, 0])
    if k % 512:
        return np.exp2(np.random.permutation(np.resize(levels, k // 32))).repeat(32)
    a = np.empty((k // 512, 16))
    for p in range(k // 512):
        a[p, :8] = np.random.permutation(np.resize(levels, 8))
        for g in range(8):
            far = levels[np.abs(levels - a[p, g]) >= 10]
            a[p, g + 8] = far[np.random.randint(len(far))]
    return np.exp2(a.ravel()).repeat(32)


def f64(x):
    return np.asarray(x).astype(np.float64)


def striped(idx):
    return np.tile(np.asarray(idx).reshape(-1, 16).T, (8, 1)).astype(np.uint16)


def unstriped(offs):
    return offs[:16].T.reshape(-1).astype(np.int64)


def striped8(idx):
    return np.asarray(idx).reshape(8, -1, 16).transpose(0, 2, 1).reshape(128, -1).astype(np.uint16)


def unstriped8(offs):
    return offs.reshape(8, 16, -1).transpose(0, 2, 1).reshape(8, -1).astype(np.int64)


def pick8(x, idx, run):
    r = np.arange(len(x))
    return x[r[:, None], idx[r % (8 * run) // run]]


E2M1 = np.array([0.0, 0.5, 1.0, 1.5, 2.0, 3.0, 4.0, 6.0, -0.0, -0.5, -1.0, -1.5, -2.0, -3.0, -4.0, -6.0])


def pack_weight(w, fmt):
    k, n = w.shape
    w = f64(np.asarray(w, np.float32).astype(ml_dtypes.bfloat16)).reshape(k // 32, 32, n)
    amax = np.abs(w).max(1)
    if fmt == "e4m3":
        byte = np.frexp(amax)[1] - 1 + 127 - 7
    else:
        mant, ex = np.frexp(amax / 6.0)
        byte = np.where(mant > 0.5, ex, ex - 1) + 127
    byte = np.clip(np.where(amax > 0, byte, 1), 1, 254)
    scaled = (w * np.exp2(127.0 - byte)[:, None, :]).reshape(k, n).astype(np.float32)
    by_word = np.ascontiguousarray(scaled.reshape(k // 512, 128, 4, n).transpose(0, 1, 3, 2))
    if fmt == "e4m3":
        words = by_word.astype(ml_dtypes.float8_e4m3fn).view(np.uint8)
    else:
        c = by_word.astype(ml_dtypes.float4_e2m1fn).view(np.uint8) & 0xF
        words = (c[..., 0::2] | (c[..., 1::2] << 4)).reshape(k // 512, 128, 2 * n)
    return np.ascontiguousarray(words), np.ascontiguousarray(byte.astype(np.uint8).reshape(k // 512, 16, n))


def unpack_weight(words, scales, fmt):
    g, _, n = scales.shape
    words = np.ascontiguousarray(words).reshape(g, 128, n, -1)
    if fmt == "e4m3":
        vals = words.view(ml_dtypes.float8_e4m3fn).astype(np.float64)
    else:
        nib = np.empty((g, 128, n, 4), np.uint8)
        nib[..., 0::2] = words & 0xF
        nib[..., 1::2] = words >> 4
        vals = E2M1[nib]
    vals = vals * np.repeat(np.exp2(scales.astype(np.float64) - 127.0), 8, axis=1)[..., None]
    return vals.transpose(0, 1, 3, 2).reshape(g * 512, n)


K, J, R, T, S, N, Z, U, E = 512, 512, 512, 2048, 256, 256, 1024, 1024, 256


def setup_inputs():
    n = np.random.standard_normal
    idx = np.random.permutation(T)[:J]
    idx2 = np.stack([np.random.permutation(J)[:S] for _ in range(8)])
    idx3 = np.stack([np.random.permutation(J)[:S] for _ in range(8)])
    idx4 = np.random.permutation(Z)[:N]
    idx5 = np.stack([np.random.permutation(U)[:J] for _ in range(8)])
    fk = mx_kscale(K)
    fr = mx_kscale(R)
    xtp = pack_weight(n((K, T)) * fk[:, None], "e4m3")
    wp = pack_weight(n((K, R)) * 1 / np.sqrt(K) / fk[:, None] * fr, "e4m3")
    w2p = pack_weight(n((K, R)) * 1 / np.sqrt(K) / fk[:, None] * fr, "e2m1")
    vsp = pack_weight(n((R, Z)) * 1 / np.sqrt(R) / fr[:, None], "e2m1")
    return {
        "xt_words": xtp[0],
        "xt_scales": xtp[1],
        "w_words": wp[0],
        "w_scales": wp[1],
        "w2_words": w2p[0],
        "w2_scales": w2p[1],
        "sa": (np.random.uniform(0.5, 1.6, (R, 1))).astype(np.float32),
        "vs_words": vsp[0],
        "vs_scales": vsp[1],
        "offs": striped(idx),
        "offs2": striped8(idx2),
        "offs3": striped8(idx3),
        "offs4": striped(idx4),
        "offs5": striped8(idx5),
    }


def reference(xt_words, xt_scales, w_words, w_scales, w2_words, w2_scales, sa, vs_words, vs_scales, offs, offs2, offs3, offs4, offs5):
    idx = unstriped(offs)
    idx2 = unstriped8(offs2)
    idx3 = unstriped8(offs3)
    idx4 = unstriped(offs4)
    idx5 = unstriped8(offs5)
    xtu = unpack_weight(xt_words, xt_scales, "e4m3")
    wu = unpack_weight(w_words, w_scales, "e4m3")
    w2u = unpack_weight(w2_words, w2_scales, "e2m1")
    vsu = unpack_weight(vs_words, vs_scales, "e2m1")
    xtidxg = xtu[:, idx]
    a = wu.T @ xtidxg
    b = w2u.T @ xtidxg
    h1 = pick8(a, idx2, 64) * f64(sa)
    pv = np.zeros((R, J))
    pv[np.arange(R)[:, None], idx3[np.arange(R) % 512 // 64]] = h1
    hid = np.abs(b - pv)
    vsidx4g = vsu[:, idx4]
    hidq = mxq(hid, 0, "e4m3")
    p = vsidx4g.T @ hidq
    m0 = np.zeros((N, U))
    m0[np.arange(N)[:, None], idx5[np.arange(N) % 128 // 16]] = p
    m1 = m0.reshape(N, E, U // E).mean(axis=2)
    m2 = np.repeat(m1, U // E, axis=1)
    y = m0 - m2
    return y

@@ -1,0 +1,242 @@
+from contextlib import ExitStack
+
+import concourse.mybir as mybir
+
+K, J, R, T, S, N, Z, U, E = 512, 512, 512, 2048, 256, 256, 1024, 1024, 256
+FLOPS = 2 * (2 * K * R * J + R * N * J)
+
+F32 = mybir.dt.float32
+BF16 = mybir.dt.bfloat16
+I32 = mybir.dt.int32
+U32 = mybir.dt.uint32
+U16 = mybir.dt.uint16
+U8 = mybir.dt.uint8
+FP8X4 = mybir.dt.float8_e4m3fn_x4
+FP4X4 = mybir.dt.float4_e2m1fn_x4
+ALU = mybir.AluOpType
+COPY = mybir.ActivationFunctionType.Copy
+AXIS_X = mybir.AxisListType.X
+
+P = 128
+PACK = 4
+QUADS = 4
+LIST_ROWS = 16
+BUCKET = U // E
+SLOT_CHUNKS = ((0, 128), (128, 256), (256, 512))
+PAGE_CHUNKS = ((0, 512), (512, 768), (768, 1024))
+
+
+def load_scale_rows(queue, plane, scales):
+    for q in range(QUADS):
+        queue.dma_start(
+            out=plane[32 * q : 32 * q + 4, :].bitcast(I32),
+            in_=scales[0, 4 * q : 4 * q + 4, :].bitcast(I32),
+        )
+
+
+def tile_picked_tokens_plain_twin_handover_store_endcontrast_kernel(
+    tc, xt_words, xt_scales, w_words, w_scales, w2_words, w2_scales, sa, vs_words, vs_scales,
+    offs, offs2, offs3, offs4, offs5, out,
+):
+    nc = tc.nc
+    with ExitStack() as ctx:
+        lists = ctx.enter_context(tc.tile_pool(name="lists", bufs=1))
+        keep = ctx.enter_context(tc.tile_pool(name="keep", bufs=1))
+        shared = ctx.enter_context(tc.tile_pool(name="shared", bufs=1))
+        psum = ctx.enter_context(tc.psum_pool(name="psum", bufs=1))
+
+        def bank(index, name):
+            return psum.tile([P, 512], F32, name=name, tag="bank%d" % index)
+
+        token_list = lists.tile([P, J // LIST_ROWS], U16)
+        take_list = lists.tile([P, S // LIST_ROWS], U16)
+        give_list = lists.tile([P, S // LIST_ROWS], U16)
+        store_list = lists.tile([P, N // LIST_ROWS], U16)
+        page_list = lists.tile([P, J // LIST_ROWS], U16)
+
+        xt_table = shared.tile([P, T], U32, offset=0)
+        xt_plane = keep.tile([P, T], U8, align_bytes=64)
+        w_raw = keep.tile([P, R], U32, align_bytes=64)
+        w_plane = keep.tile([P, R], U8, align_bytes=64)
+        w2_raw = keep.tile([P, R], U16, align_bytes=64)
+        w2_plane = keep.tile([P, R], U8, align_bytes=64)
+        vs_table = keep.tile([P, Z], U16, align_bytes=64)
+        vs_plane = keep.tile([P, Z], U8, align_bytes=64)
+        weight = keep.tile([P, PACK], F32)
+
+        w_rows = keep.tile([PACK, QUADS, R // 4], I32, align_bytes=64)
+        nc.vector.memset(xt_plane[:].bitcast(I32), 0)
+        for plane in (w_plane, w2_plane, vs_plane):
+            nc.gpsimd.memset(plane[:].bitcast(I32), 0)
+
+        nc.sync.dma_start(token_list[:], offs)
+        nc.sync.dma_start(out=xt_table[:].bitcast(I32), in_=xt_words[0].rearrange("p c t -> p (c t)").bitcast(I32))
+        nc.scalar.dma_start(out=w_rows[:], in_=w_scales[0].bitcast(I32).rearrange("(q i) c -> i q c", i=PACK))
+        load_scale_rows(nc.scalar, xt_plane, xt_scales)
+        nc.sync.dma_start(out=w_raw[:].bitcast(I32), in_=w_words[0].rearrange("p c t -> p (c t)").bitcast(I32))
+        nc.sync.dma_start(take_list[:], offs2)
+        nc.sync.dma_start(give_list[:], offs3)
+        nc.sync.dma_start(out=weight[:], in_=sa.rearrange("(p t) o -> p (t o)", t=PACK))
+        nc.sync.dma_start(out=w2_raw[:].bitcast(I32), in_=w2_words[0].bitcast(I32))
+        load_scale_rows(nc.sync, w2_plane, w2_scales)
+        nc.sync.dma_start(store_list[:], offs4)
+        nc.sync.dma_start(out=vs_table[:].bitcast(I32), in_=vs_words[0].bitcast(I32))
+        load_scale_rows(nc.sync, vs_plane, vs_scales)
+        nc.sync.dma_start(page_list[:], offs5)
+
+        handed = [keep.tile([P, J], F32, name="handed%d" % t) for t in range(PACK)]
+        for t in range(PACK):
+            nc.gpsimd.memset(handed[t][:], 0.0)
+
+        w_codes = [keep.tile([P, P], U32, name="w_codes%d" % t, align_bytes=64) for t in range(1)]
+        w_bytes = keep.tile([P, PACK, P], U8, align_bytes=64)
+        w_codes_rest = keep.tile([P, PACK - 1, P], U32, align_bytes=64)
+        x_codes = keep.tile([P, J], U32, align_bytes=64)
+        x_bytes = keep.tile([P, J], U8, align_bytes=64)
+
+        for q in range(QUADS):
+            nc.vector.tensor_copy(w_plane[32 * q : 32 * q + 4, :].bitcast(I32), w_rows[:, q, :])
+        nc.vector.tensor_copy(w_bytes[:], w_plane[:].rearrange("p (m t) -> p t m", t=PACK))
+        nc.vector.tensor_copy(x_bytes[:], xt_plane[:].indirect(token_list[:]))
+        half = J // 2
+
+        def gather_tokens(h):
+            nc.vector.tensor_copy(
+                x_codes[:, h * half : (h + 1) * half],
+                xt_table[:].indirect(token_list[:, h * half // LIST_ROWS : (h + 1) * half // LIST_ROWS]),
+            )
+
+        gather_tokens(0)
+        nc.vector.tensor_copy(w_codes[0][:].bitcast(I32), w_raw[:].bitcast(I32).rearrange("p (m t) -> p t m", t=PACK)[:, 0, :])
+        gather_tokens(1)
+        nc.vector.tensor_copy(w_codes_rest[:].bitcast(I32), w_raw[:].bitcast(I32).rearrange("p (m t) -> p t m", t=PACK)[:, 1:, :])
+
+        first = [keep.tile([P, J], F32, name="first%d" % t) for t in range(PACK)]
+        for h in range(2):
+            cols = slice(h * half, (h + 1) * half)
+            acc = bank(h, "a0_%d" % h)
+            nc.tensor.matmul_mx(
+                out=acc[:, :half], lhsT=w_codes[0][:].bitcast(FP8X4), lhsT_scale=w_bytes[:, 0, :],
+                rhs=x_codes[:, cols].bitcast(FP8X4), rhs_scale=x_bytes[:, cols], start=True, stop=True,
+            )
+            nc.scalar.activation(first[0][:, cols], acc[:, :half], COPY)
+        for t in range(1, PACK):
+            acc = bank(1 + t, "a%d" % t)
+            nc.tensor.matmul_mx(
+                out=acc[:], lhsT=w_codes_rest[:, t - 1, :].bitcast(FP8X4), lhsT_scale=w_bytes[:, t, :],
+                rhs=x_codes[:].bitcast(FP8X4), rhs_scale=x_bytes[:], start=True, stop=True,
+            )
+            nc.vector.tensor_copy(first[t][:], acc[:])
+
+        parcels = [keep.tile([P, S], F32, name="parcels%d" % t) for t in range(PACK)]
+
+        def take(t):
+            nc.scalar.activation(parcels[t][:], first[t][:].indirect(take_list[:]), COPY, scale=weight[:, t : t + 1])
+
+        def give(t):
+            nc.scalar.activation(handed[t][:].indirect(give_list[:]), parcels[t][:], COPY)
+
+        take(0)
+        for t in range(PACK):
+            if t + 1 < PACK:
+                take(t + 1)
+            give(t)
+
+        w2_codes = keep.tile([P, PACK, P], U16, align_bytes=64)
+        w2_bytes = keep.tile([P, PACK, P], U8, align_bytes=64)
+        nc.gpsimd.tensor_copy(
+            w2_codes[:].bitcast(U8).rearrange("p t (m b) -> p t m b", b=2),
+            w2_raw[:].bitcast(U8).rearrange("p (m t b) -> p t m b", t=PACK, b=2),
+        )
+        nc.gpsimd.tensor_copy(w2_bytes[:], w2_plane[:].rearrange("p (m t) -> p t m", t=PACK))
+
+        second_banks = (5, 0, 1, 6)
+        second = []
+        for t in range(PACK):
+            acc = bank(second_banks[t], "b%d" % t)
+            nc.tensor.matmul_mx(
+                out=acc[:], lhsT=w2_codes[:, t, :].bitcast(FP4X4), lhsT_scale=w2_bytes[:, t, :],
+                rhs=x_codes[:].bitcast(FP8X4), rhs_scale=x_bytes[:], start=True, stop=True,
+            )
+            second.append(acc)
+
+        v_codes = keep.tile([P, N], U16, align_bytes=64)
+        v_bytes = keep.tile([P, N], U8, align_bytes=64)
+        nc.vector.tensor_copy(v_codes[:], vs_table[:].indirect(store_list[:]))
+        nc.vector.tensor_copy(v_bytes[:], vs_plane[:].indirect(store_list[:]))
+
+        pages = [shared.tile([P, U], F32, name="page%d" % m, offset=m * U * 4) for m in range(N // P)]
+        for m in range(N // P):
+            nc.gpsimd.memset(pages[m][:], 0.0)
+
+        diff = [keep.tile([P, 2, J], F32, name="diff%d" % u) for u in range(2)]
+        hidden = keep.tile([P, J, PACK], BF16, align_bytes=64)
+
+        def subtract(t, cols):
+            nc.vector.tensor_tensor(diff[t // 2][:, t % 2, cols], second[t][:, cols], handed[t][:, cols], ALU.subtract)
+
+        def magnitude(u, cols):
+            pair = diff[u][:, :, cols].rearrange("p t j -> p j t")
+            nc.vector.scalar_tensor_tensor(
+                out=hidden[:, cols, 2 * u : 2 * u + 2], in0=pair, scalar=-1.0, in1=pair, op0=ALU.mult, op1=ALU.max,
+            )
+
+        every = slice(0, J)
+        subtract(0, every)
+        subtract(1, every)
+        magnitude(0, every)
+        subtract(2, every)
+
+        h_codes = keep.tile([P, J], U32, align_bytes=64)
+        h_bytes = keep.tile([P, J], U8, align_bytes=64)
+        results = [keep.tile([P, J], F32, name="results%d" % m) for m in range(N // P)]
+        result_banks = ((2, 3), (4, 7), (5, 0))
+        for c, (j0, j1) in enumerate(SLOT_CHUNKS):
+            cols = slice(j0, j1)
+            subtract(3, cols)
+            magnitude(1, cols)
+            nc.vector.quantize_mx(
+                out=h_codes[:, cols].bitcast(FP8X4), scales=h_bytes[:, cols],
+                in_=hidden[:, cols, :].rearrange("p j t -> p (j t)"),
+            )
+            for m in range(N // P):
+                acc = bank(result_banks[c][m], "p%d_%d" % (c, m))
+                rows = slice(m * P, (m + 1) * P)
+                nc.tensor.matmul_mx(
+                    out=acc[:, : j1 - j0], lhsT=v_codes[:, rows].bitcast(FP4X4), lhsT_scale=v_bytes[:, rows],
+                    rhs=h_codes[:, cols].bitcast(FP8X4), rhs_scale=h_bytes[:, cols], start=True, stop=True,
+                )
+                if c == 0:
+                    nc.scalar.copy(results[m][:, cols], acc[:, : j1 - j0])
+                else:
+                    nc.vector.tensor_copy(results[m][:, cols], acc[:, : j1 - j0])
+
+        def put(m, j0, j1):
+            nc.scalar.activation(
+                pages[m][:].indirect(page_list[:, j0 // LIST_ROWS : j1 // LIST_ROWS]), results[m][:, j0:j1], COPY,
+            )
+
+        put(0, 0, 128)
+        put(1, 0, 128)
+        put(0, 128, 256)
+        put(0, 256, 512)
+        put(1, 128, 512)
+
+        for m in range(N // P):
+            sums = keep.tile([P, E], F32, name="sums%d" % m)
+            final = keep.tile([P, U], F32, name="final%d" % m)
+            for u0, u1 in ((0, 512), (512, 1024)):
+                nc.vector.tensor_reduce(
+                    out=sums[:, u0 // BUCKET : u1 // BUCKET],
+                    in_=pages[m][:, u0:u1].rearrange("p (e c) -> p e c", c=BUCKET), axis=AXIS_X, op=ALU.add,
+                )
+            for u0, u1 in PAGE_CHUNKS:
+                buckets = (u1 - u0) // BUCKET
+                nc.vector.scalar_tensor_tensor(
+                    out=final[:, u0:u1].rearrange("p (e c) -> p e c", c=BUCKET),
+                    in0=sums[:, u0 // BUCKET : u1 // BUCKET].unsqueeze(2).to_broadcast([P, buckets, BUCKET]),
+                    scalar=-1.0 / BUCKET,
+                    in1=pages[m][:, u0:u1].rearrange("p (e c) -> p e c", c=BUCKET),
+                    op0=ALU.mult, op1=ALU.add,
+                )
+                nc.sync.dma_start(out=out[m * P : (m + 1) * P, u0:u1], in_=final[:, u0:u1])

@@ -15,6 +15,7 @@ FP8X4 = mybir.dt.float8_e4m3fn_x4
 FP4X4 = mybir.dt.float4_e2m1fn_x4
 ALU = mybir.AluOpType
 COPY = mybir.ActivationFunctionType.Copy
+ABS = mybir.ActivationFunctionType.Abs
 AXIS_X = mybir.AxisListType.X
 
 P = 128
@@ -22,6 +23,7 @@ PACK = 4
 QUADS = 4
 LIST_ROWS = 16
 BUCKET = U // E
+TOKEN_CHUNKS = ((0, 256), (256, 384), (384, 512))
 SLOT_CHUNKS = ((0, 128), (128, 256), (256, 512))
 PAGE_CHUNKS = ((0, 512), (512, 768), (768, 1024))
 
@@ -54,20 +56,19 @@ def tile_picked_tokens_plain_twin_handover_store_endcontrast_kernel(
         store_list = lists.tile([P, N // LIST_ROWS], U16)
         page_list = lists.tile([P, J // LIST_ROWS], U16)
 
-        xt_table = shared.tile([P, T], U32, offset=0)
+        xt_table = shared.tile([P, T], U32, align_bytes=64, offset=0)
         xt_plane = keep.tile([P, T], U8, align_bytes=64)
         w_raw = keep.tile([P, R], U32, align_bytes=64)
         w_plane = keep.tile([P, R], U8, align_bytes=64)
         w2_raw = keep.tile([P, R], U16, align_bytes=64)
         w2_plane = keep.tile([P, R], U8, align_bytes=64)
-        vs_table = keep.tile([P, Z], U16, align_bytes=64)
-        vs_plane = keep.tile([P, Z], U8, align_bytes=64)
+        vs_table = shared.tile([P, Z], U16, align_bytes=64, offset=20480)
+        vs_plane = shared.tile([P, Z], U8, align_bytes=64, offset=22528)
         weight = keep.tile([P, PACK], F32)
 
         w_rows = keep.tile([PACK, QUADS, R // 4], I32, align_bytes=64)
-        nc.vector.memset(xt_plane[:].bitcast(I32), 0)
-        for plane in (w_plane, w2_plane, vs_plane):
-            nc.gpsimd.memset(plane[:].bitcast(I32), 0)
+        for plane in (xt_plane, w_plane, w2_plane, vs_plane):
+            nc.vector.memset(plane[:].bitcast(I32), 0)
 
         nc.sync.dma_start(token_list[:], offs)
         nc.sync.dma_start(out=xt_table[:].bitcast(I32), in_=xt_words[0].rearrange("p c t -> p (c t)").bitcast(I32))
@@ -84,13 +85,8 @@ def tile_picked_tokens_plain_twin_handover_store_endcontrast_kernel(
         load_scale_rows(nc.sync, vs_plane, vs_scales)
         nc.sync.dma_start(page_list[:], offs5)
 
-        handed = [keep.tile([P, J], F32, name="handed%d" % t) for t in range(PACK)]
-        for t in range(PACK):
-            nc.gpsimd.memset(handed[t][:], 0.0)
-
-        w_codes = [keep.tile([P, P], U32, name="w_codes%d" % t, align_bytes=64) for t in range(1)]
-        w_bytes = keep.tile([P, PACK, P], U8, align_bytes=64)
-        w_codes_rest = keep.tile([P, PACK - 1, P], U32, align_bytes=64)
+        w_codes = shared.tile([P, PACK, P], U32, align_bytes=64, offset=16384)
+        w_bytes = shared.tile([P, PACK, P], U8, align_bytes=64, offset=18432)
         x_codes = keep.tile([P, J], U32, align_bytes=64)
         x_bytes = keep.tile([P, J], U8, align_bytes=64)
 
@@ -98,32 +94,34 @@ def tile_picked_tokens_plain_twin_handover_store_endcontrast_kernel(
             nc.vector.tensor_copy(w_plane[32 * q : 32 * q + 4, :].bitcast(I32), w_rows[:, q, :])
         nc.vector.tensor_copy(w_bytes[:], w_plane[:].rearrange("p (m t) -> p t m", t=PACK))
         nc.vector.tensor_copy(x_bytes[:], xt_plane[:].indirect(token_list[:]))
-        half = J // 2
 
-        def gather_tokens(h):
-            nc.vector.tensor_copy(
-                x_codes[:, h * half : (h + 1) * half],
-                xt_table[:].indirect(token_list[:, h * half // LIST_ROWS : (h + 1) * half // LIST_ROWS]),
-            )
+        def gather_tokens(j0, j1):
+            nc.vector.tensor_copy(x_codes[:, j0:j1], xt_table[:].indirect(token_list[:, j0 // LIST_ROWS : j1 // LIST_ROWS]))
 
-        gather_tokens(0)
-        nc.vector.tensor_copy(w_codes[0][:].bitcast(I32), w_raw[:].bitcast(I32).rearrange("p (m t) -> p t m", t=PACK)[:, 0, :])
-        gather_tokens(1)
-        nc.vector.tensor_copy(w_codes_rest[:].bitcast(I32), w_raw[:].bitcast(I32).rearrange("p (m t) -> p t m", t=PACK)[:, 1:, :])
+        w_dealt = w_raw[:].bitcast(I32).rearrange("p (m t) -> p t m", t=PACK)
+        gather_tokens(*TOKEN_CHUNKS[0])
+        nc.vector.tensor_copy(w_codes[:, 0, :].bitcast(I32), w_dealt[:, 0, :])
+        for j0, j1 in TOKEN_CHUNKS[1:]:
+            gather_tokens(j0, j1)
+        nc.vector.tensor_copy(w_codes[:, 1:, :].bitcast(I32), w_dealt[:, 1:, :])
 
-        first = [keep.tile([P, J], F32, name="first%d" % t) for t in range(PACK)]
-        for h in range(2):
-            cols = slice(h * half, (h + 1) * half)
-            acc = bank(h, "a0_%d" % h)
+        handed = [shared.tile([P, J], F32, name="handed%d" % t, align_bytes=64, offset=2048 * t) for t in range(PACK)]
+        for t in range(PACK):
+            nc.gpsimd.memset(handed[t][:], 0.0)
+
+        first = [shared.tile([P, J], F32, name="first%d" % t, align_bytes=64, offset=8192 + 2048 * t) for t in range(PACK)]
+        for h, (j0, j1) in enumerate(TOKEN_CHUNKS):
+            cols = slice(j0, j1)
+            acc = bank((0, 1, 7)[h], "a0_%d" % h)
             nc.tensor.matmul_mx(
-                out=acc[:, :half], lhsT=w_codes[0][:].bitcast(FP8X4), lhsT_scale=w_bytes[:, 0, :],
+                out=acc[:, : j1 - j0], lhsT=w_codes[:, 0, :].bitcast(FP8X4), lhsT_scale=w_bytes[:, 0, :],
                 rhs=x_codes[:, cols].bitcast(FP8X4), rhs_scale=x_bytes[:, cols], start=True, stop=True,
             )
-            nc.scalar.activation(first[0][:, cols], acc[:, :half], COPY)
+            nc.scalar.activation(first[0][:, cols], acc[:, : j1 - j0], COPY)
         for t in range(1, PACK):
             acc = bank(1 + t, "a%d" % t)
             nc.tensor.matmul_mx(
-                out=acc[:], lhsT=w_codes_rest[:, t - 1, :].bitcast(FP8X4), lhsT_scale=w_bytes[:, t, :],
+                out=acc[:], lhsT=w_codes[:, t, :].bitcast(FP8X4), lhsT_scale=w_bytes[:, t, :],
                 rhs=x_codes[:].bitcast(FP8X4), rhs_scale=x_bytes[:], start=True, stop=True,
             )
             nc.vector.tensor_copy(first[t][:], acc[:])
@@ -137,18 +135,20 @@ def tile_picked_tokens_plain_twin_handover_store_endcontrast_kernel(
             nc.scalar.activation(handed[t][:].indirect(give_list[:]), parcels[t][:], COPY)
 
         take(0)
-        for t in range(PACK):
+        give(0)
+        take(1)
+        for t in range(1, PACK):
             if t + 1 < PACK:
                 take(t + 1)
             give(t)
 
-        w2_codes = keep.tile([P, PACK, P], U16, align_bytes=64)
-        w2_bytes = keep.tile([P, PACK, P], U8, align_bytes=64)
-        nc.gpsimd.tensor_copy(
+        w2_codes = shared.tile([P, PACK, P], U16, align_bytes=64, offset=16384)
+        w2_bytes = shared.tile([P, PACK, P], U8, align_bytes=64, offset=18432)
+        nc.vector.tensor_copy(
             w2_codes[:].bitcast(U8).rearrange("p t (m b) -> p t m b", b=2),
             w2_raw[:].bitcast(U8).rearrange("p (m t b) -> p t m b", t=PACK, b=2),
         )
-        nc.gpsimd.tensor_copy(w2_bytes[:], w2_plane[:].rearrange("p (m t) -> p t m", t=PACK))
+        nc.vector.tensor_copy(w2_bytes[:], w2_plane[:].rearrange("p (m t) -> p t m", t=PACK))
 
         second_banks = (5, 0, 1, 6)
         second = []
@@ -165,27 +165,31 @@ def tile_picked_tokens_plain_twin_handover_store_endcontrast_kernel(
         nc.vector.tensor_copy(v_codes[:], vs_table[:].indirect(store_list[:]))
         nc.vector.tensor_copy(v_bytes[:], vs_plane[:].indirect(store_list[:]))
 
-        pages = [shared.tile([P, U], F32, name="page%d" % m, offset=m * U * 4) for m in range(N // P)]
+        pages = [shared.tile([P, U], F32, name="page%d" % m, align_bytes=64, offset=8192 + m * U * 4) for m in range(N // P)]
         for m in range(N // P):
             nc.gpsimd.memset(pages[m][:], 0.0)
 
-        diff = [keep.tile([P, 2, J], F32, name="diff%d" % u) for u in range(2)]
         hidden = keep.tile([P, J, PACK], BF16, align_bytes=64)
 
-        def subtract(t, cols):
-            nc.vector.tensor_tensor(diff[t // 2][:, t % 2, cols], second[t][:, cols], handed[t][:, cols], ALU.subtract)
+        def subtract(t, cols, into):
+            nc.vector.tensor_tensor(into, second[t][:, cols], handed[t][:, cols], ALU.subtract)
 
-        def magnitude(u, cols):
-            pair = diff[u][:, :, cols].rearrange("p t j -> p j t")
-            nc.vector.scalar_tensor_tensor(
-                out=hidden[:, cols, 2 * u : 2 * u + 2], in0=pair, scalar=-1.0, in1=pair, op0=ALU.mult, op1=ALU.max,
-            )
+        def magnitude_on_vector(pair, into):
+            pair = pair.rearrange("p t j -> p j t")
+            nc.vector.scalar_tensor_tensor(out=into, in0=pair, scalar=-1.0, in1=pair, op0=ALU.mult, op1=ALU.max)
 
-        every = slice(0, J)
-        subtract(0, every)
-        subtract(1, every)
-        magnitude(0, every)
-        subtract(2, every)
+        low_pair = shared.tile([P, 2, J], F32, align_bytes=64, offset=20480)
+        for t in range(2):
+            subtract(t, slice(0, J), low_pair[:, t, :])
+        magnitude_on_vector(low_pair[:], hidden[:, :, 0:2])
+
+        high = shared.tile([P, 768], F32, align_bytes=64, offset=20480)
+        starts = (256, 512, 0)
+        high_pair = [
+            high[:, s0 : s0 + 2 * (j1 - j0)].rearrange("p (t j) -> p t j", t=2) for s0, (j0, j1) in zip(starts, SLOT_CHUNKS)
+        ]
+        for c, (j0, j1) in enumerate(SLOT_CHUNKS):
+            subtract(2, slice(j0, j1), high_pair[c][:, 0, :])
 
         h_codes = keep.tile([P, J], U32, align_bytes=64)
         h_bytes = keep.tile([P, J], U8, align_bytes=64)
@@ -193,12 +197,17 @@ def tile_picked_tokens_plain_twin_handover_store_endcontrast_kernel(
         result_banks = ((2, 3), (4, 7), (5, 0))
         for c, (j0, j1) in enumerate(SLOT_CHUNKS):
             cols = slice(j0, j1)
-            subtract(3, cols)
-            magnitude(1, cols)
+            subtract(3, cols, high_pair[c][:, 1, :])
+            if c < 2:
+                nc.scalar.activation(hidden[:, cols, 2:4], high_pair[c].rearrange("p t j -> p j t"), ABS)
+            else:
+                magnitude_on_vector(high_pair[c], hidden[:, cols, 2:4])
             nc.vector.quantize_mx(
                 out=h_codes[:, cols].bitcast(FP8X4), scales=h_bytes[:, cols],
                 in_=hidden[:, cols, :].rearrange("p j t -> p (j t)"),
             )
+        for c, (j0, j1) in enumerate(SLOT_CHUNKS):
+            cols = slice(j0, j1)
             for m in range(N // P):
                 acc = bank(result_banks[c][m], "p%d_%d" % (c, m))
                 rows = slice(m * P, (m + 1) * P)

@@ -57,7 +57,7 @@ def tile_picked_tokens_plain_twin_handover_store_endcontrast_kernel(
         page_list = lists.tile([P, J // LIST_ROWS], U16)
 
         xt_table = shared.tile([P, T], U32, align_bytes=64, offset=0)
-        xt_plane = keep.tile([P, T], U8, align_bytes=64)
+        xt_plane = shared.tile([P, T], U8, align_bytes=64, offset=24576)
         w_raw = keep.tile([P, R], U32, align_bytes=64)
         w_plane = keep.tile([P, R], U8, align_bytes=64)
         w2_raw = keep.tile([P, R], U16, align_bytes=64)
@@ -66,16 +66,17 @@ def tile_picked_tokens_plain_twin_handover_store_endcontrast_kernel(
         vs_plane = shared.tile([P, Z], U8, align_bytes=64, offset=22528)
         weight = keep.tile([P, PACK], F32)
 
+        xt_rows = keep.tile([PACK, QUADS, T // 4], I32, align_bytes=64)
         w_rows = keep.tile([PACK, QUADS, R // 4], I32, align_bytes=64)
         for plane in (xt_plane, w_plane, w2_plane, vs_plane):
             nc.vector.memset(plane[:].bitcast(I32), 0)
 
         nc.sync.dma_start(token_list[:], offs)
-        nc.sync.dma_start(out=xt_table[:].bitcast(I32), in_=xt_words[0].rearrange("p c t -> p (c t)").bitcast(I32))
-        nc.scalar.dma_start(out=w_rows[:], in_=w_scales[0].bitcast(I32).rearrange("(q i) c -> i q c", i=PACK))
-        load_scale_rows(nc.scalar, xt_plane, xt_scales)
-        nc.sync.dma_start(out=w_raw[:].bitcast(I32), in_=w_words[0].rearrange("p c t -> p (c t)").bitcast(I32))
         nc.sync.dma_start(take_list[:], offs2)
+        nc.sync.dma_start(out=xt_table[:].bitcast(I32), in_=xt_words[0].rearrange("p c t -> p (c t)").bitcast(I32))
+        nc.scalar.dma_start(out=xt_rows[:], in_=xt_scales[0].bitcast(I32).rearrange("(q i) c -> i q c", i=PACK))
+        nc.scalar.dma_start(out=w_rows[:], in_=w_scales[0].bitcast(I32).rearrange("(q i) c -> i q c", i=PACK))
+        nc.sync.dma_start(out=w_raw[:].bitcast(I32), in_=w_words[0].rearrange("p c t -> p (c t)").bitcast(I32))
         nc.sync.dma_start(give_list[:], offs3)
         nc.sync.dma_start(out=weight[:], in_=sa.rearrange("(p t) o -> p (t o)", t=PACK))
         nc.sync.dma_start(out=w2_raw[:].bitcast(I32), in_=w2_words[0].bitcast(I32))
@@ -87,23 +88,22 @@ def tile_picked_tokens_plain_twin_handover_store_endcontrast_kernel(
 
         w_codes = shared.tile([P, PACK, P], U32, align_bytes=64, offset=16384)
         w_bytes = shared.tile([P, PACK, P], U8, align_bytes=64, offset=18432)
-        x_codes = keep.tile([P, J], U32, align_bytes=64)
+        x_codes = shared.tile([P, J], U32, align_bytes=64, offset=24576)
         x_bytes = keep.tile([P, J], U8, align_bytes=64)
 
         for q in range(QUADS):
+            nc.vector.tensor_copy(xt_plane[32 * q : 32 * q + 4, :].bitcast(I32), xt_rows[:, q, :])
             nc.vector.tensor_copy(w_plane[32 * q : 32 * q + 4, :].bitcast(I32), w_rows[:, q, :])
-        nc.vector.tensor_copy(w_bytes[:], w_plane[:].rearrange("p (m t) -> p t m", t=PACK))
         nc.vector.tensor_copy(x_bytes[:], xt_plane[:].indirect(token_list[:]))
 
         def gather_tokens(j0, j1):
             nc.vector.tensor_copy(x_codes[:, j0:j1], xt_table[:].indirect(token_list[:, j0 // LIST_ROWS : j1 // LIST_ROWS]))
 
-        w_dealt = w_raw[:].bitcast(I32).rearrange("p (m t) -> p t m", t=PACK)
         gather_tokens(*TOKEN_CHUNKS[0])
-        nc.vector.tensor_copy(w_codes[:, 0, :].bitcast(I32), w_dealt[:, 0, :])
+        nc.scalar.copy(w_codes[:].rearrange("p t m -> p m t"), w_raw[:].rearrange("p (m t) -> p m t", t=PACK))
+        nc.gpsimd.tensor_copy(w_bytes[:], w_plane[:].rearrange("p (m t) -> p t m", t=PACK))
         for j0, j1 in TOKEN_CHUNKS[1:]:
             gather_tokens(j0, j1)
-        nc.vector.tensor_copy(w_codes[:, 1:, :].bitcast(I32), w_dealt[:, 1:, :])
 
         handed = [shared.tile([P, J], F32, name="handed%d" % t, align_bytes=64, offset=2048 * t) for t in range(PACK)]
         for t in range(PACK):
@@ -145,10 +145,10 @@ def tile_picked_tokens_plain_twin_handover_store_endcontrast_kernel(
         w2_codes = shared.tile([P, PACK, P], U16, align_bytes=64, offset=16384)
         w2_bytes = shared.tile([P, PACK, P], U8, align_bytes=64, offset=18432)
         nc.vector.tensor_copy(
-            w2_codes[:].bitcast(U8).rearrange("p t (m b) -> p t m b", b=2),
-            w2_raw[:].bitcast(U8).rearrange("p (m t b) -> p t m b", t=PACK, b=2),
+            w2_codes[:].bitcast(U8).rearrange("p t (m b) -> p m t b", b=2),
+            w2_raw[:].bitcast(U8).rearrange("p (m t b) -> p m t b", t=PACK, b=2),
         )
-        nc.vector.tensor_copy(w2_bytes[:], w2_plane[:].rearrange("p (m t) -> p t m", t=PACK))
+        nc.vector.tensor_copy(w2_bytes[:].rearrange("p t m -> p m t"), w2_plane[:].rearrange("p (m t) -> p m t", t=PACK))
 
         second_banks = (5, 0, 1, 6)
         second = []
@@ -232,7 +232,7 @@ def tile_picked_tokens_plain_twin_handover_store_endcontrast_kernel(
         put(1, 128, 512)
 
         for m in range(N // P):
-            sums = keep.tile([P, E], F32, name="sums%d" % m)
+            sums = keep.tile([P, E], F32, name="sums%d" % m, tag="sums")
             final = keep.tile([P, U], F32, name="final%d" % m)
             for u0, u1 in ((0, 512), (512, 1024)):
                 nc.vector.tensor_reduce(

@@ -66,33 +66,31 @@ def tile_picked_tokens_plain_twin_handover_store_endcontrast_kernel(
         vs_plane = shared.tile([P, Z], U8, align_bytes=64, offset=22528)
         weight = keep.tile([P, PACK], F32)
 
-        xt_rows = keep.tile([PACK, QUADS, T // 4], I32, align_bytes=64)
         w_rows = keep.tile([PACK, QUADS, R // 4], I32, align_bytes=64)
         for plane in (xt_plane, w_plane, w2_plane, vs_plane):
             nc.vector.memset(plane[:].bitcast(I32), 0)
 
         nc.sync.dma_start(token_list[:], offs)
-        nc.sync.dma_start(take_list[:], offs2)
         nc.sync.dma_start(out=xt_table[:].bitcast(I32), in_=xt_words[0].rearrange("p c t -> p (c t)").bitcast(I32))
-        nc.scalar.dma_start(out=xt_rows[:], in_=xt_scales[0].bitcast(I32).rearrange("(q i) c -> i q c", i=PACK))
         nc.scalar.dma_start(out=w_rows[:], in_=w_scales[0].bitcast(I32).rearrange("(q i) c -> i q c", i=PACK))
+        load_scale_rows(nc.scalar, xt_plane, xt_scales)
         nc.sync.dma_start(out=w_raw[:].bitcast(I32), in_=w_words[0].rearrange("p c t -> p (c t)").bitcast(I32))
+        nc.sync.dma_start(out=w2_raw[:].bitcast(I32), in_=w2_words[0].bitcast(I32))
+        nc.sync.dma_start(take_list[:], offs2)
         nc.sync.dma_start(give_list[:], offs3)
         nc.sync.dma_start(out=weight[:], in_=sa.rearrange("(p t) o -> p (t o)", t=PACK))
-        nc.sync.dma_start(out=w2_raw[:].bitcast(I32), in_=w2_words[0].bitcast(I32))
         load_scale_rows(nc.sync, w2_plane, w2_scales)
         nc.sync.dma_start(store_list[:], offs4)
         nc.sync.dma_start(out=vs_table[:].bitcast(I32), in_=vs_words[0].bitcast(I32))
         load_scale_rows(nc.sync, vs_plane, vs_scales)
         nc.sync.dma_start(page_list[:], offs5)
 
-        w_codes = shared.tile([P, PACK, P], U32, align_bytes=64, offset=16384)
-        w_bytes = shared.tile([P, PACK, P], U8, align_bytes=64, offset=18432)
+        w_codes = keep.tile([P, PACK, P], U32, align_bytes=64)
+        w_bytes = keep.tile([P, PACK, P], U8, align_bytes=64)
         x_codes = shared.tile([P, J], U32, align_bytes=64, offset=24576)
         x_bytes = keep.tile([P, J], U8, align_bytes=64)
 
         for q in range(QUADS):
-            nc.vector.tensor_copy(xt_plane[32 * q : 32 * q + 4, :].bitcast(I32), xt_rows[:, q, :])
             nc.vector.tensor_copy(w_plane[32 * q : 32 * q + 4, :].bitcast(I32), w_rows[:, q, :])
         nc.vector.tensor_copy(x_bytes[:], xt_plane[:].indirect(token_list[:]))
 
@@ -102,6 +100,8 @@ def tile_picked_tokens_plain_twin_handover_store_endcontrast_kernel(
         gather_tokens(*TOKEN_CHUNKS[0])
         nc.scalar.copy(w_codes[:].rearrange("p t m -> p m t"), w_raw[:].rearrange("p (m t) -> p m t", t=PACK))
         nc.gpsimd.tensor_copy(w_bytes[:], w_plane[:].rearrange("p (m t) -> p t m", t=PACK))
+        w2_codes = keep.tile([P, PACK, P], U16, align_bytes=64)
+        nc.scalar.copy(w2_codes[:].rearrange("p t m -> p m t"), w2_raw[:].rearrange("p (m t) -> p m t", t=PACK))
         for j0, j1 in TOKEN_CHUNKS[1:]:
             gather_tokens(j0, j1)
 
@@ -142,13 +142,8 @@ def tile_picked_tokens_plain_twin_handover_store_endcontrast_kernel(
                 take(t + 1)
             give(t)
 
-        w2_codes = shared.tile([P, PACK, P], U16, align_bytes=64, offset=16384)
-        w2_bytes = shared.tile([P, PACK, P], U8, align_bytes=64, offset=18432)
-        nc.vector.tensor_copy(
-            w2_codes[:].bitcast(U8).rearrange("p t (m b) -> p m t b", b=2),
-            w2_raw[:].bitcast(U8).rearrange("p (m t b) -> p m t b", t=PACK, b=2),
-        )
-        nc.vector.tensor_copy(w2_bytes[:].rearrange("p t m -> p m t"), w2_plane[:].rearrange("p (m t) -> p m t", t=PACK))
+        w2_bytes = keep.tile([P, PACK, P], U8, align_bytes=64)
+        nc.gpsimd.tensor_copy(w2_bytes[:], w2_plane[:].rearrange("p (m t) -> p t m", t=PACK))
 
         second_banks = (5, 0, 1, 6)
         second = []

from contextlib import ExitStack

import concourse.mybir as mybir

K, J, R, T, S, N, Z, U, E = 512, 512, 512, 2048, 256, 256, 1024, 1024, 256
FLOPS = 2 * (2 * K * R * J + R * N * J)

F32 = mybir.dt.float32
BF16 = mybir.dt.bfloat16
I32 = mybir.dt.int32
U32 = mybir.dt.uint32
U16 = mybir.dt.uint16
U8 = mybir.dt.uint8
FP8X4 = mybir.dt.float8_e4m3fn_x4
FP4X4 = mybir.dt.float4_e2m1fn_x4
ALU = mybir.AluOpType
COPY = mybir.ActivationFunctionType.Copy
ABS = mybir.ActivationFunctionType.Abs
AXIS_X = mybir.AxisListType.X

P = 128
PACK = 4
QUADS = 4
LIST_ROWS = 16
BUCKET = U // E
TOKEN_CHUNKS = ((0, 256), (256, 384), (384, 512))
SLOT_CHUNKS = ((0, 128), (128, 256), (256, 512))
PAGE_CHUNKS = ((0, 512), (512, 768), (768, 1024))


def load_scale_rows(queue, plane, scales):
    for q in range(QUADS):
        queue.dma_start(
            out=plane[32 * q : 32 * q + 4, :].bitcast(I32),
            in_=scales[0, 4 * q : 4 * q + 4, :].bitcast(I32),
        )


def tile_picked_tokens_plain_twin_handover_store_endcontrast_kernel(
    tc, xt_words, xt_scales, w_words, w_scales, w2_words, w2_scales, sa, vs_words, vs_scales,
    offs, offs2, offs3, offs4, offs5, out,
):
    nc = tc.nc
    with ExitStack() as ctx:
        lists = ctx.enter_context(tc.tile_pool(name="lists", bufs=1))
        keep = ctx.enter_context(tc.tile_pool(name="keep", bufs=1))
        shared = ctx.enter_context(tc.tile_pool(name="shared", bufs=1))
        psum = ctx.enter_context(tc.psum_pool(name="psum", bufs=1))

        def bank(index, name):
            return psum.tile([P, 512], F32, name=name, tag="bank%d" % index)

        token_list = lists.tile([P, J // LIST_ROWS], U16)
        take_list = lists.tile([P, S // LIST_ROWS], U16)
        give_list = lists.tile([P, S // LIST_ROWS], U16)
        store_list = lists.tile([P, N // LIST_ROWS], U16)
        page_list = lists.tile([P, J // LIST_ROWS], U16)

        xt_table = shared.tile([P, T], U32, align_bytes=64, offset=0)
        xt_plane = shared.tile([P, T], U8, align_bytes=64, offset=24576)
        w_raw = keep.tile([P, R], U32, align_bytes=64)
        w_plane = keep.tile([P, R], U8, align_bytes=64)
        w2_raw = keep.tile([P, R], U16, align_bytes=64)
        w2_plane = keep.tile([P, R], U8, align_bytes=64)
        vs_table = shared.tile([P, Z], U16, align_bytes=64, offset=20480)
        vs_plane = shared.tile([P, Z], U8, align_bytes=64, offset=22528)
        weight = keep.tile([P, PACK], F32)

        w_rows = keep.tile([PACK, QUADS, R // 4], I32, align_bytes=64)
        for plane in (xt_plane, w_plane, w2_plane, vs_plane):
            nc.vector.memset(plane[:].bitcast(I32), 0)

        nc.sync.dma_start(token_list[:], offs)
        nc.sync.dma_start(out=xt_table[:].bitcast(I32), in_=xt_words[0].rearrange("p c t -> p (c t)").bitcast(I32))
        nc.scalar.dma_start(out=w_rows[:], in_=w_scales[0].bitcast(I32).rearrange("(q i) c -> i q c", i=PACK))
        load_scale_rows(nc.scalar, xt_plane, xt_scales)
        nc.sync.dma_start(out=w_raw[:].bitcast(I32), in_=w_words[0].rearrange("p c t -> p (c t)").bitcast(I32))
        nc.sync.dma_start(out=w2_raw[:].bitcast(I32), in_=w2_words[0].bitcast(I32))
        nc.sync.dma_start(take_list[:], offs2)
        nc.sync.dma_start(give_list[:], offs3)
        nc.sync.dma_start(out=weight[:], in_=sa.rearrange("(p t) o -> p (t o)", t=PACK))
        load_scale_rows(nc.sync, w2_plane, w2_scales)
        nc.sync.dma_start(store_list[:], offs4)
        nc.sync.dma_start(out=vs_table[:].bitcast(I32), in_=vs_words[0].bitcast(I32))
        load_scale_rows(nc.sync, vs_plane, vs_scales)
        nc.sync.dma_start(page_list[:], offs5)

        w_codes = keep.tile([P, PACK, P], U32, align_bytes=64)
        w_bytes = keep.tile([P, PACK, P], U8, align_bytes=64)
        x_codes = shared.tile([P, J], U32, align_bytes=64, offset=24576)
        x_bytes = keep.tile([P, J], U8, align_bytes=64)

        for q in range(QUADS):
            nc.vector.tensor_copy(w_plane[32 * q : 32 * q + 4, :].bitcast(I32), w_rows[:, q, :])
        nc.vector.tensor_copy(x_bytes[:], xt_plane[:].indirect(token_list[:]))

        def gather_tokens(j0, j1):
            nc.vector.tensor_copy(x_codes[:, j0:j1], xt_table[:].indirect(token_list[:, j0 // LIST_ROWS : j1 // LIST_ROWS]))

        gather_tokens(*TOKEN_CHUNKS[0])
        nc.scalar.copy(w_codes[:].rearrange("p t m -> p m t"), w_raw[:].rearrange("p (m t) -> p m t", t=PACK))
        nc.gpsimd.tensor_copy(w_bytes[:], w_plane[:].rearrange("p (m t) -> p t m", t=PACK))
        w2_codes = keep.tile([P, PACK, P], U16, align_bytes=64)
        nc.scalar.copy(w2_codes[:].rearrange("p t m -> p m t"), w2_raw[:].rearrange("p (m t) -> p m t", t=PACK))
        for j0, j1 in TOKEN_CHUNKS[1:]:
            gather_tokens(j0, j1)

        handed = [shared.tile([P, J], F32, name="handed%d" % t, align_bytes=64, offset=2048 * t) for t in range(PACK)]
        for t in range(PACK):
            nc.gpsimd.memset(handed[t][:], 0.0)

        first = [shared.tile([P, J], F32, name="first%d" % t, align_bytes=64, offset=8192 + 2048 * t) for t in range(PACK)]
        for h, (j0, j1) in enumerate(TOKEN_CHUNKS):
            cols = slice(j0, j1)
            acc = bank((0, 1, 7)[h], "a0_%d" % h)
            nc.tensor.matmul_mx(
                out=acc[:, : j1 - j0], lhsT=w_codes[:, 0, :].bitcast(FP8X4), lhsT_scale=w_bytes[:, 0, :],
                rhs=x_codes[:, cols].bitcast(FP8X4), rhs_scale=x_bytes[:, cols], start=True, stop=True,
            )
            nc.scalar.activation(first[0][:, cols], acc[:, : j1 - j0], COPY)
        for t in range(1, PACK):
            acc = bank(1 + t, "a%d" % t)
            nc.tensor.matmul_mx(
                out=acc[:], lhsT=w_codes[:, t, :].bitcast(FP8X4), lhsT_scale=w_bytes[:, t, :],
                rhs=x_codes[:].bitcast(FP8X4), rhs_scale=x_bytes[:], start=True, stop=True,
            )
            nc.vector.tensor_copy(first[t][:], acc[:])

        parcels = [keep.tile([P, S], F32, name="parcels%d" % t) for t in range(PACK)]

        def take(t):
            nc.scalar.activation(parcels[t][:], first[t][:].indirect(take_list[:]), COPY, scale=weight[:, t : t + 1])

        def give(t):
            nc.scalar.activation(handed[t][:].indirect(give_list[:]), parcels[t][:], COPY)

        take(0)
        give(0)
        take(1)
        for t in range(1, PACK):
            if t + 1 < PACK:
                take(t + 1)
            give(t)

        w2_bytes = keep.tile([P, PACK, P], U8, align_bytes=64)
        nc.gpsimd.tensor_copy(w2_bytes[:], w2_plane[:].rearrange("p (m t) -> p t m", t=PACK))

        second_banks = (5, 0, 1, 6)
        second = []
        for t in range(PACK):
            acc = bank(second_banks[t], "b%d" % t)
            nc.tensor.matmul_mx(
                out=acc[:], lhsT=w2_codes[:, t, :].bitcast(FP4X4), lhsT_scale=w2_bytes[:, t, :],
                rhs=x_codes[:].bitcast(FP8X4), rhs_scale=x_bytes[:], start=True, stop=True,
            )
            second.append(acc)

        v_codes = keep.tile([P, N], U16, align_bytes=64)
        v_bytes = keep.tile([P, N], U8, align_bytes=64)
        nc.vector.tensor_copy(v_codes[:], vs_table[:].indirect(store_list[:]))
        nc.vector.tensor_copy(v_bytes[:], vs_plane[:].indirect(store_list[:]))

        pages = [shared.tile([P, U], F32, name="page%d" % m, align_bytes=64, offset=8192 + m * U * 4) for m in range(N // P)]
        for m in range(N // P):
            nc.gpsimd.memset(pages[m][:], 0.0)

        hidden = keep.tile([P, J, PACK], BF16, align_bytes=64)

        def subtract(t, cols, into):
            nc.vector.tensor_tensor(into, second[t][:, cols], handed[t][:, cols], ALU.subtract)

        def magnitude_on_vector(pair, into):
            pair = pair.rearrange("p t j -> p j t")
            nc.vector.scalar_tensor_tensor(out=into, in0=pair, scalar=-1.0, in1=pair, op0=ALU.mult, op1=ALU.max)

        low_pair = shared.tile([P, 2, J], F32, align_bytes=64, offset=20480)
        for t in range(2):
            subtract(t, slice(0, J), low_pair[:, t, :])
        magnitude_on_vector(low_pair[:], hidden[:, :, 0:2])

        high = shared.tile([P, 768], F32, align_bytes=64, offset=20480)
        starts = (256, 512, 0)
        high_pair = [
            high[:, s0 : s0 + 2 * (j1 - j0)].rearrange("p (t j) -> p t j", t=2) for s0, (j0, j1) in zip(starts, SLOT_CHUNKS)
        ]
        for c, (j0, j1) in enumerate(SLOT_CHUNKS):
            subtract(2, slice(j0, j1), high_pair[c][:, 0, :])

        h_codes = keep.tile([P, J], U32, align_bytes=64)
        h_bytes = keep.tile([P, J], U8, align_bytes=64)
        results = [keep.tile([P, J], F32, name="results%d" % m) for m in range(N // P)]
        result_banks = ((2, 3), (4, 7), (5, 0))
        for c, (j0, j1) in enumerate(SLOT_CHUNKS):
            cols = slice(j0, j1)
            subtract(3, cols, high_pair[c][:, 1, :])
            if c < 2:
                nc.scalar.activation(hidden[:, cols, 2:4], high_pair[c].rearrange("p t j -> p j t"), ABS)
            else:
                magnitude_on_vector(high_pair[c], hidden[:, cols, 2:4])
            nc.vector.quantize_mx(
                out=h_codes[:, cols].bitcast(FP8X4), scales=h_bytes[:, cols],
                in_=hidden[:, cols, :].rearrange("p j t -> p (j t)"),
            )
        for c, (j0, j1) in enumerate(SLOT_CHUNKS):
            cols = slice(j0, j1)
            for m in range(N // P):
                acc = bank(result_banks[c][m], "p%d_%d" % (c, m))
                rows = slice(m * P, (m + 1) * P)
                nc.tensor.matmul_mx(
                    out=acc[:, : j1 - j0], lhsT=v_codes[:, rows].bitcast(FP4X4), lhsT_scale=v_bytes[:, rows],
                    rhs=h_codes[:, cols].bitcast(FP8X4), rhs_scale=h_bytes[:, cols], start=True, stop=True,
                )
                if c == 0:
                    nc.scalar.copy(results[m][:, cols], acc[:, : j1 - j0])
                else:
                    nc.vector.tensor_copy(results[m][:, cols], acc[:, : j1 - j0])

        def put(m, j0, j1):
            nc.scalar.activation(
                pages[m][:].indirect(page_list[:, j0 // LIST_ROWS : j1 // LIST_ROWS]), results[m][:, j0:j1], COPY,
            )

        put(0, 0, 128)
        put(1, 0, 128)
        put(0, 128, 256)
        put(0, 256, 512)
        put(1, 128, 512)

        for m in range(N // P):
            sums = keep.tile([P, E], F32, name="sums%d" % m, tag="sums")
            final = keep.tile([P, U], F32, name="final%d" % m)
            for u0, u1 in ((0, 512), (512, 1024)):
                nc.vector.tensor_reduce(
                    out=sums[:, u0 // BUCKET : u1 // BUCKET],
                    in_=pages[m][:, u0:u1].rearrange("p (e c) -> p e c", c=BUCKET), axis=AXIS_X, op=ALU.add,
                )
            for u0, u1 in PAGE_CHUNKS:
                buckets = (u1 - u0) // BUCKET
                nc.vector.scalar_tensor_tensor(
                    out=final[:, u0:u1].rearrange("p (e c) -> p e c", c=BUCKET),
                    in0=sums[:, u0 // BUCKET : u1 // BUCKET].unsqueeze(2).to_broadcast([P, buckets, BUCKET]),
                    scalar=-1.0 / BUCKET,
                    in1=pages[m][:, u0:u1].rearrange("p (e c) -> p e c", c=BUCKET),
                    op0=ALU.mult, op1=ALU.add,
                )
                nc.sync.dma_start(out=out[m * P : (m + 1) * P, u0:u1], in_=final[:, u0:u1])
